import numpy as np
import ml_dtypes


def mxq(x, axis, fmt="e4m3"):
    dtype, down = {"e4m3": (ml_dtypes.float8_e4m3fn, 7), "e5m2": (ml_dtypes.float8_e5m2, 14)}[fmt]
    v = np.moveaxis(np.asarray(x, np.float32).astype(ml_dtypes.bfloat16).astype(np.float64), axis, -1)
    blocks = v.reshape(v.shape[:-1] + (-1, 32))
    amax = np.abs(blocks).max(-1, keepdims=True)
    byte = np.maximum(np.where(amax > 0, np.frexp(amax)[1] - 1 + 127, 0) - down, 1)
    scale = np.exp2(byte - 127.0)
    codes = (blocks / scale).astype(np.float32).astype(dtype).astype(np.float64)
    return np.moveaxis((codes * scale).reshape(v.shape), -1, axis)


WIDE = False


def mx_kscale(k):
    if not WIDE:
        return np.ones(k)
    levels = np.array([10, -10, 5, -5, 0])
    if k % 512:
        return np.exp2(np.random.permutation(np.resize(levels, k // 32))).repeat(32)
    a = np.empty((k // 512, 16))
    for p in range(k // 512):
        a[p, :8] = np.random.permutation(np.resize(levels, 8))
        for g in range(8):
            far = levels[np.abs(levels - a[p, g]) >= 10]
            a[p, g + 8] = far[np.random.randint(len(far))]
    return np.exp2(a.ravel()).repeat(32)


def f64(x):
    return np.asarray(x).astype(np.float64)


def striped(idx):
    return np.tile(idx.reshape(-1, 16).T, (8, 1)).astype(np.uint16)


def unstriped(offs):
    return offs[:16].T.reshape(-1).astype(np.int64)


def pack_weight(w):
    k, n = w.shape
    w = f64(np.asarray(w, np.float32).astype(ml_dtypes.bfloat16)).reshape(k // 32, 32, n)
    amax = np.abs(w).max(1)
    byte = np.clip(np.where(amax > 0, np.frexp(amax)[1] - 1 + 127 - 7, 1), 1, 254)
    scaled = (w * np.exp2(127.0 - byte)[:, None, :]).reshape(k, n).astype(np.float32)
    words = np.ascontiguousarray(scaled.reshape(k // 512, 128, 4, n).transpose(0, 1, 3, 2)).astype(ml_dtypes.float8_e4m3fn).view(np.uint8)
    return words, np.ascontiguousarray(byte.astype(np.uint8).reshape(k // 512, 16, n))


def unpack_weight(words, scales):
    g, p, n, _ = words.shape
    vals = np.ascontiguousarray(words).view(ml_dtypes.float8_e4m3fn).astype(np.float64) * np.repeat(np.exp2(scales.astype(np.float64) - 127.0), 8, axis=1)[..., None]
    return vals.transpose(0, 1, 3, 2).reshape(g * 512, n)


E2M1 = np.array([0.0, 0.5, 1.0, 1.5, 2.0, 3.0, 4.0, 6.0, -0.0, -0.5, -1.0, -1.5, -2.0, -3.0, -4.0, -6.0])


def pack_fp4(w):
    k, n = w.shape
    w = f64(np.asarray(w, np.float32).astype(ml_dtypes.bfloat16)).reshape(k // 32, 32, n)
    amax = np.abs(w).max(1)
    mant, ex = np.frexp(amax / 6.0)
    byte = np.clip(np.where(amax > 0, np.where(mant > 0.5, ex, ex - 1) + 127, 1), 1, 254)
    scaled = (w * np.exp2(127.0 - byte)[:, None, :]).reshape(k, n).astype(np.float32)
    c = np.ascontiguousarray(scaled.reshape(k // 512, 128, 4, n).transpose(0, 1, 3, 2)).astype(ml_dtypes.float4_e2m1fn).view(np.uint8) & 0xF
    words = (c[..., 0::2] | (c[..., 1::2] << 4)).reshape(k // 512, 128, 2 * n)
    return np.ascontiguousarray(words), np.ascontiguousarray(byte.astype(np.uint8).reshape(k // 512, 16, n))


def unpack_fp4(words, scales):
    g, _, n = scales.shape
    words = np.ascontiguousarray(words).reshape(g, 128, n, 2)
    nib = np.empty((g, 128, n, 4), np.uint8)
    nib[..., 0::2] = words & 0xF
    nib[..., 1::2] = words >> 4
    vals = E2M1[nib] * np.repeat(np.exp2(scales.astype(np.float64) - 127.0), 8, axis=1)[..., None]
    return vals.transpose(0, 1, 3, 2).reshape(g * 512, n)


K, T, S, N, G, H, U = 512, 2048, 256, 512, 2048, 512, 512


def setup_inputs():
    n = np.random.standard_normal
    s = mx_kscale(K)[:, None]
    u = mx_kscale(K)
    packed_xT = pack_weight(n((K, T)) * s)
    packed_dT = pack_weight(n((K, G)) / s)
    packed_w1 = pack_fp4(n((H, N)) / np.sqrt(H) / u[:, None])
    perm = np.random.permutation(U)
    return {
        "x_words": packed_xT[0],
        "x_scales": packed_xT[1],
        "d_words": packed_dT[0],
        "d_scales": packed_dT[1],
        "gn": (np.random.uniform(0.5, 1.5, (H, 1)) * u[:, None]).astype(np.float32),
        "w1_words": packed_w1[0],
        "w1_scales": packed_w1[1],
        "offs": striped(np.random.permutation(T)[:S]),
        "ci": striped(np.random.permutation(G)[:H]),
        "n1": striped(perm[:S]),
        "n2": striped(perm[S:]),
        "n3": striped(np.random.permutation(U)),
    }


def reference(x_words, x_scales, d_words, d_scales, gn, w1_words, w1_scales, offs, ci, n1, n2, n3):
    d_ci = unpack_weight(d_words, d_scales)[:, unstriped(ci)]
    xq = unpack_weight(x_words, x_scales)[:, unstriped(offs)]
    s = 0.0625 * (d_ci.T @ xq)
    z = f64(gn) * s
    h = unpack_fp4(w1_words, w1_scales).T @ mxq(z, 0, "e4m3")
    nw = 0.5 * h
    ph = np.zeros((N, U))
    ph[:, unstriped(n1)] = h
    pg = ph.copy()
    pg[:, unstriped(n2)] = nw
    return pg - pg[:, unstriped(n3)]

@@ -1,0 +1,176 @@
+from contextlib import ExitStack
+
+import concourse.mybir as mybir
+
+F32 = mybir.dt.float32
+BF16 = mybir.dt.bfloat16
+I32 = mybir.dt.int32
+U32 = mybir.dt.uint32
+U16 = mybir.dt.uint16
+U8 = mybir.dt.uint8
+FP8X4 = mybir.dt.float8_e4m3fn_x4
+FP4X4 = mybir.dt.float4_e2m1fn_x4
+COPY = mybir.ActivationFunctionType.Copy
+MULT = mybir.AluOpType.mult
+SUBTRACT = mybir.AluOpType.subtract
+
+P = 128
+PACK = 4
+TABLE = 2048
+TOKENS = 256
+CODEWORDS = 512
+ROWS = 512
+SLOTS = 512
+HALF = TOKENS // 2
+BLOCKS = ROWS // P
+PER_COLUMN = 16
+X_PLANE = 4
+D_PLANE = 8
+
+FLOPS = 2 * 512 * CODEWORDS * TOKENS + 2 * CODEWORDS * ROWS * TOKENS
+
+
+def load_scale_rows(queue, plane, first, rows):
+    for r in range(PACK):
+        queue.dma_start(out=plane[first + r : P : 32, :].bitcast(I32), in_=rows[r::PACK, :].bitcast(I32))
+
+
+def entries(offsets, start, count):
+    return offsets[:, start // PER_COLUMN : (start + count) // PER_COLUMN]
+
+
+def tile_picked_dwlipagtwo_none_p_kernel(
+    tc, x_words, x_scales, d_words, d_scales, gn, w1_words, w1_scales, offs, ci, n1, n2, n3, out
+):
+    nc = tc.nc
+    with ExitStack() as ctx:
+        keep = ctx.enter_context(tc.tile_pool(name="keep", bufs=1))
+        psum = ctx.enter_context(tc.psum_pool(name="psum", bufs=1))
+
+        ci_list = keep.tile([P, CODEWORDS // PER_COLUMN], U16, name="ci_list")
+        offs_list = keep.tile([P, TOKENS // PER_COLUMN], U16, name="offs_list")
+        n1_list = keep.tile([P, TOKENS // PER_COLUMN], U16, name="n1_list")
+        n2_list = keep.tile([P, TOKENS // PER_COLUMN], U16, name="n2_list")
+        n3_list = keep.tile([P, SLOTS // PER_COLUMN], U16, name="n3_list")
+        d_table = keep.tile([P, TABLE], I32, name="d_table", align_bytes=64)
+        x_table = keep.tile([P, TABLE], I32, name="x_table", align_bytes=64)
+        d_scale_table = keep.tile([P, TABLE], U8, name="d_scale_table", align_bytes=64)
+        x_scale_table = keep.tile([P, TABLE], U8, name="x_scale_table", align_bytes=64)
+        w_codes = keep.tile([P, 2 * ROWS], U8, name="w_codes", align_bytes=64)
+        w_plane = keep.tile([P, ROWS], U8, name="w_plane", align_bytes=64)
+        gain = keep.tile([P, PACK], F32, name="gain")
+        gain16 = keep.tile([P, PACK], F32, name="gain16")
+        pages = [keep.tile([P, SLOTS], F32, name="page%d" % b, align_bytes=64) for b in range(BLOCKS)]
+
+        nc.vector.memset(d_scale_table[:].bitcast(I32), 0)
+        nc.vector.memset(x_scale_table[:].bitcast(I32), 0)
+        nc.vector.memset(w_plane[:].bitcast(I32), 0)
+        for page in pages:
+            nc.vector.memset(page[:], 0.0)
+
+        nc.gpsimd.dma_start(out=gain[:], in_=gn.rearrange("(p t) o -> p (t o)", t=PACK))
+        load_scale_rows(nc.scalar, d_scale_table, D_PLANE, d_scales[0])
+        nc.sync.dma_start(ci_list[:], ci)
+        nc.sync.dma_start(offs_list[:], offs)
+        nc.sync.dma_start(out=d_table[:], in_=d_words[0].rearrange("p n t -> p (n t)").bitcast(I32))
+        load_scale_rows(nc.sync, x_scale_table, X_PLANE, x_scales[0])
+        nc.sync.dma_start(out=x_table[:], in_=x_words[0].rearrange("p n t -> p (n t)").bitcast(I32))
+        nc.sync.dma_start(out=w_codes[:].bitcast(I32), in_=w1_words[0].bitcast(I32))
+        load_scale_rows(nc.sync, w_plane, 0, w1_scales[0])
+        nc.sync.dma_start(n1_list[:], n1)
+        nc.sync.dma_start(n2_list[:], n2)
+        nc.sync.dma_start(n3_list[:], n3)
+
+        nc.scalar.activation(out=gain16[:], in_=gain[:], func=COPY, scale=0.0625)
+
+        d_plane = keep.tile([P, CODEWORDS], U8, name="d_plane", align_bytes=64)
+        d_codes = keep.tile([P, CODEWORDS], U32, name="d_codes", align_bytes=64)
+        x_plane = keep.tile([P, TOKENS], U8, name="x_plane", align_bytes=64)
+        x_codes = [keep.tile([P, HALF], U32, name="x_codes%d" % u, align_bytes=64) for u in range(2)]
+        nc.vector.tensor_copy(
+            out=d_plane[:].rearrange("p (t m) -> p m t", t=PACK), in_=d_scale_table[:].indirect(ci_list[:])
+        )
+        nc.vector.tensor_copy(
+            out=d_codes[:].rearrange("p (t m) -> p m t", t=PACK), in_=d_table[:].bitcast(U32).indirect(ci_list[:])
+        )
+        nc.vector.tensor_copy(out=x_plane[:], in_=x_scale_table[:].indirect(offs_list[:]))
+        for u in range(2):
+            nc.vector.tensor_copy(
+                out=x_codes[u][:], in_=x_table[:].bitcast(U32).indirect(entries(offs_list, u * HALF, HALF))
+            )
+
+        z_codes = keep.tile([P, TOKENS], U32, name="z_codes", align_bytes=64)
+        z_plane = keep.tile([P, TOKENS], U8, name="z_plane", align_bytes=64)
+        h_rows = [keep.tile([P, TOKENS], F32, name="h_rows%d" % b, align_bytes=64) for b in range(BLOCKS)]
+
+        def layer(b, start, count, name):
+            h_bank = psum.tile([P, count], F32, name=name)
+            nc.tensor.matmul_mx(
+                out=h_bank[:],
+                lhsT=w_codes[:, 2 * P * b : 2 * P * (b + 1)].bitcast(FP4X4),
+                lhsT_scale=w_plane[:, P * b : P * (b + 1)],
+                rhs=z_codes[:, start : start + count].bitcast(FP8X4),
+                rhs_scale=z_plane[:, start : start + count],
+                start=True,
+                stop=True,
+            )
+            nc.vector.tensor_copy(out=h_rows[b][:, start : start + count], in_=h_bank[:])
+
+        for u in range(2):
+            tokens = slice(u * HALF, (u + 1) * HALF)
+            s_bank = psum.tile([P, PACK, HALF], F32, name="s_bank%d" % u)
+            for t in range(PACK):
+                nc.tensor.matmul_mx(
+                    out=s_bank[:, t, :],
+                    lhsT=d_codes[:, t * P : (t + 1) * P].bitcast(FP8X4),
+                    lhsT_scale=d_plane[D_PLANE:P, t * P : (t + 1) * P],
+                    rhs=x_codes[u][:].bitcast(FP8X4),
+                    rhs_scale=x_plane[X_PLANE:P, tokens],
+                    start=True,
+                    stop=True,
+                )
+            z_half = keep.tile([P, HALF, PACK], BF16, name="z_half%d" % u, align_bytes=64)
+            nc.vector.tensor_tensor(
+                out=z_half[:],
+                in0=s_bank[:].rearrange("p t j -> p j t"),
+                in1=gain16[:].unsqueeze(1).to_broadcast([P, HALF, PACK]),
+                op=MULT,
+            )
+            nc.vector.quantize_mx(
+                out=z_codes[:, tokens].bitcast(FP8X4),
+                scales=z_plane[:, tokens],
+                in_=z_half[:].rearrange("p j t -> p (j t)"),
+            )
+            for b in (0, 1):
+                layer(b, u * HALF, HALF, "h_bank%d_%d" % (b, u))
+        for b in (2, 3):
+            layer(b, 0, TOKENS, "h_bank%d" % b)
+
+        def scatter(pair, start, count):
+            for offsets, factor in ((n1_list, 1.0), (n2_list, 0.5)):
+                for b in pair:
+                    nc.scalar.activation(
+                        out=pages[b][:].indirect(entries(offsets, start, count)),
+                        in_=h_rows[b][:, start : start + count],
+                        func=COPY,
+                        scale=factor,
+                    )
+
+        def finish(b):
+            for v in range(2):
+                slots = slice(v * SLOTS // 2, (v + 1) * SLOTS // 2)
+                fetched = keep.tile([P, SLOTS // 2], F32, name="fetched%d_%d" % (b, v), align_bytes=64)
+                nc.scalar.activation(
+                    out=fetched[:], in_=pages[b][:].indirect(entries(n3_list, v * SLOTS // 2, SLOTS // 2)), func=COPY
+                )
+                result = keep.tile([P, SLOTS // 2], F32, name="result%d_%d" % (b, v), align_bytes=64)
+                nc.vector.tensor_tensor(out=result[:], in0=pages[b][:, slots], in1=fetched[:], op=SUBTRACT)
+                nc.sync.dma_start(out=out[b * P : (b + 1) * P, slots], in_=result[:])
+
+        scatter((0, 1), 0, HALF)
+        scatter((0, 1), HALF, HALF)
+        finish(0)
+        finish(1)
+        scatter((2, 3), 0, TOKENS)
+        finish(2)
+        finish(3)

@@ -26,6 +26,7 @@ BLOCKS = ROWS // P
 PER_COLUMN = 16
 X_PLANE = 4
 D_PLANE = 8
+D_LEAD = 512
 
 FLOPS = 2 * 512 * CODEWORDS * TOKENS + 2 * CODEWORDS * ROWS * TOKENS
 
@@ -65,14 +66,14 @@ def tile_picked_dwlipagtwo_none_p_kernel(
         nc.vector.memset(d_scale_table[:].bitcast(I32), 0)
         nc.vector.memset(x_scale_table[:].bitcast(I32), 0)
         nc.vector.memset(w_plane[:].bitcast(I32), 0)
-        for page in pages:
-            nc.vector.memset(page[:], 0.0)
 
+        d_source = d_words[0].rearrange("p n t -> p (n t)").bitcast(I32)
         nc.gpsimd.dma_start(out=gain[:], in_=gn.rearrange("(p t) o -> p (t o)", t=PACK))
-        load_scale_rows(nc.scalar, d_scale_table, D_PLANE, d_scales[0])
         nc.sync.dma_start(ci_list[:], ci)
+        nc.sync.dma_start(out=d_table[:, :D_LEAD], in_=d_source[:, :D_LEAD])
+        load_scale_rows(nc.sync, d_scale_table, D_PLANE, d_scales[0])
+        nc.sync.dma_start(out=d_table[:, D_LEAD:], in_=d_source[:, D_LEAD:])
         nc.sync.dma_start(offs_list[:], offs)
-        nc.sync.dma_start(out=d_table[:], in_=d_words[0].rearrange("p n t -> p (n t)").bitcast(I32))
         load_scale_rows(nc.sync, x_scale_table, X_PLANE, x_scales[0])
         nc.sync.dma_start(out=x_table[:], in_=x_words[0].rearrange("p n t -> p (n t)").bitcast(I32))
         nc.sync.dma_start(out=w_codes[:].bitcast(I32), in_=w1_words[0].bitcast(I32))
@@ -86,7 +87,6 @@ def tile_picked_dwlipagtwo_none_p_kernel(
         d_plane = keep.tile([P, CODEWORDS], U8, name="d_plane", align_bytes=64)
         d_codes = keep.tile([P, CODEWORDS], U32, name="d_codes", align_bytes=64)
         x_plane = keep.tile([P, TOKENS], U8, name="x_plane", align_bytes=64)
-        x_codes = [keep.tile([P, HALF], U32, name="x_codes%d" % u, align_bytes=64) for u in range(2)]
         nc.vector.tensor_copy(
             out=d_plane[:].rearrange("p (t m) -> p m t", t=PACK), in_=d_scale_table[:].indirect(ci_list[:])
         )
@@ -94,17 +94,13 @@ def tile_picked_dwlipagtwo_none_p_kernel(
             out=d_codes[:].rearrange("p (t m) -> p m t", t=PACK), in_=d_table[:].bitcast(U32).indirect(ci_list[:])
         )
         nc.vector.tensor_copy(out=x_plane[:], in_=x_scale_table[:].indirect(offs_list[:]))
-        for u in range(2):
-            nc.vector.tensor_copy(
-                out=x_codes[u][:], in_=x_table[:].bitcast(U32).indirect(entries(offs_list, u * HALF, HALF))
-            )
 
         z_codes = keep.tile([P, TOKENS], U32, name="z_codes", align_bytes=64)
         z_plane = keep.tile([P, TOKENS], U8, name="z_plane", align_bytes=64)
         h_rows = [keep.tile([P, TOKENS], F32, name="h_rows%d" % b, align_bytes=64) for b in range(BLOCKS)]
 
-        def layer(b, start, count, name):
-            h_bank = psum.tile([P, count], F32, name=name)
+        def layer(b, start, count, bank):
+            h_bank = psum.tile([P, count], F32, name="h_bank%d_%d" % (b, start), tag=bank)
             nc.tensor.matmul_mx(
                 out=h_bank[:],
                 lhsT=w_codes[:, 2 * P * b : 2 * P * (b + 1)].bitcast(FP4X4),
@@ -118,13 +114,17 @@ def tile_picked_dwlipagtwo_none_p_kernel(
 
         for u in range(2):
             tokens = slice(u * HALF, (u + 1) * HALF)
-            s_bank = psum.tile([P, PACK, HALF], F32, name="s_bank%d" % u)
+            x_codes = keep.tile([P, HALF], U32, name="x_codes%d" % u, align_bytes=64)
+            nc.vector.tensor_copy(
+                out=x_codes[:], in_=x_table[:].bitcast(U32).indirect(entries(offs_list, u * HALF, HALF))
+            )
+            s_bank = psum.tile([P, PACK, HALF], F32, name="s_bank%d" % u, tag="bank%d" % u)
             for t in range(PACK):
                 nc.tensor.matmul_mx(
                     out=s_bank[:, t, :],
                     lhsT=d_codes[:, t * P : (t + 1) * P].bitcast(FP8X4),
                     lhsT_scale=d_plane[D_PLANE:P, t * P : (t + 1) * P],
-                    rhs=x_codes[u][:].bitcast(FP8X4),
+                    rhs=x_codes[:].bitcast(FP8X4),
                     rhs_scale=x_plane[X_PLANE:P, tokens],
                     start=True,
                     stop=True,
@@ -142,9 +142,9 @@ def tile_picked_dwlipagtwo_none_p_kernel(
                 in_=z_half[:].rearrange("p j t -> p (j t)"),
             )
             for b in (0, 1):
-                layer(b, u * HALF, HALF, "h_bank%d_%d" % (b, u))
+                layer(b, u * HALF, HALF, "bank%d" % (1 + 2 * u + b))
         for b in (2, 3):
-            layer(b, 0, TOKENS, "h_bank%d" % b)
+            layer(b, 0, TOKENS, "bank%d" % (3 + b))
 
         def scatter(pair, start, count):
             for offsets, factor in ((n1_list, 1.0), (n2_list, 0.5)):
@@ -156,21 +156,23 @@ def tile_picked_dwlipagtwo_none_p_kernel(
                         scale=factor,
                     )
 
-        def finish(b):
-            for v in range(2):
-                slots = slice(v * SLOTS // 2, (v + 1) * SLOTS // 2)
-                fetched = keep.tile([P, SLOTS // 2], F32, name="fetched%d_%d" % (b, v), align_bytes=64)
+        def finish(b, widths):
+            start = 0
+            for width in widths:
+                slots = slice(start, start + width)
+                fetched = keep.tile([P, width], F32, name="fetched%d_%d" % (b, start), align_bytes=64)
                 nc.scalar.activation(
-                    out=fetched[:], in_=pages[b][:].indirect(entries(n3_list, v * SLOTS // 2, SLOTS // 2)), func=COPY
+                    out=fetched[:], in_=pages[b][:].indirect(entries(n3_list, start, width)), func=COPY
                 )
-                result = keep.tile([P, SLOTS // 2], F32, name="result%d_%d" % (b, v), align_bytes=64)
+                result = keep.tile([P, width], F32, name="result%d_%d" % (b, start), align_bytes=64)
                 nc.vector.tensor_tensor(out=result[:], in0=pages[b][:, slots], in1=fetched[:], op=SUBTRACT)
                 nc.sync.dma_start(out=out[b * P : (b + 1) * P, slots], in_=result[:])
+                start += width
 
         scatter((0, 1), 0, HALF)
         scatter((0, 1), HALF, HALF)
-        finish(0)
-        finish(1)
+        finish(0, (256, 256))
+        finish(1, (256, 256))
         scatter((2, 3), 0, TOKENS)
-        finish(2)
-        finish(3)
+        finish(2, (256, 256))
+        finish(3, (256, 128, 128))

from contextlib import ExitStack

import concourse.mybir as mybir

F32 = mybir.dt.float32
BF16 = mybir.dt.bfloat16
I32 = mybir.dt.int32
U32 = mybir.dt.uint32
U16 = mybir.dt.uint16
U8 = mybir.dt.uint8
FP8X4 = mybir.dt.float8_e4m3fn_x4
FP4X4 = mybir.dt.float4_e2m1fn_x4
COPY = mybir.ActivationFunctionType.Copy
MULT = mybir.AluOpType.mult
SUBTRACT = mybir.AluOpType.subtract

P = 128
PACK = 4
TABLE = 2048
TOKENS = 256
CODEWORDS = 512
ROWS = 512
SLOTS = 512
HALF = TOKENS // 2
BLOCKS = ROWS // P
PER_COLUMN = 16
X_PLANE = 4
D_PLANE = 8
D_LEAD = 512

FLOPS = 2 * 512 * CODEWORDS * TOKENS + 2 * CODEWORDS * ROWS * TOKENS


def load_scale_rows(queue, plane, first, rows):
    for r in range(PACK):
        queue.dma_start(out=plane[first + r : P : 32, :].bitcast(I32), in_=rows[r::PACK, :].bitcast(I32))


def entries(offsets, start, count):
    return offsets[:, start // PER_COLUMN : (start + count) // PER_COLUMN]


def tile_picked_dwlipagtwo_none_p_kernel(
    tc, x_words, x_scales, d_words, d_scales, gn, w1_words, w1_scales, offs, ci, n1, n2, n3, out
):
    nc = tc.nc
    with ExitStack() as ctx:
        keep = ctx.enter_context(tc.tile_pool(name="keep", bufs=1))
        psum = ctx.enter_context(tc.psum_pool(name="psum", bufs=1))

        ci_list = keep.tile([P, CODEWORDS // PER_COLUMN], U16, name="ci_list")
        offs_list = keep.tile([P, TOKENS // PER_COLUMN], U16, name="offs_list")
        n1_list = keep.tile([P, TOKENS // PER_COLUMN], U16, name="n1_list")
        n2_list = keep.tile([P, TOKENS // PER_COLUMN], U16, name="n2_list")
        n3_list = keep.tile([P, SLOTS // PER_COLUMN], U16, name="n3_list")
        d_table = keep.tile([P, TABLE], I32, name="d_table", align_bytes=64)
        x_table = keep.tile([P, TABLE], I32, name="x_table", align_bytes=64)
        d_scale_table = keep.tile([P, TABLE], U8, name="d_scale_table", align_bytes=64)
        x_scale_table = keep.tile([P, TABLE], U8, name="x_scale_table", align_bytes=64)
        w_codes = keep.tile([P, 2 * ROWS], U8, name="w_codes", align_bytes=64)
        w_plane = keep.tile([P, ROWS], U8, name="w_plane", align_bytes=64)
        gain = keep.tile([P, PACK], F32, name="gain")
        gain16 = keep.tile([P, PACK], F32, name="gain16")
        pages = [keep.tile([P, SLOTS], F32, name="page%d" % b, align_bytes=64) for b in range(BLOCKS)]

        nc.vector.memset(d_scale_table[:].bitcast(I32), 0)
        nc.vector.memset(x_scale_table[:].bitcast(I32), 0)
        nc.vector.memset(w_plane[:].bitcast(I32), 0)

        d_source = d_words[0].rearrange("p n t -> p (n t)").bitcast(I32)
        nc.gpsimd.dma_start(out=gain[:], in_=gn.rearrange("(p t) o -> p (t o)", t=PACK))
        nc.sync.dma_start(ci_list[:], ci)
        nc.sync.dma_start(out=d_table[:, :D_LEAD], in_=d_source[:, :D_LEAD])
        load_scale_rows(nc.sync, d_scale_table, D_PLANE, d_scales[0])
        nc.sync.dma_start(out=d_table[:, D_LEAD:], in_=d_source[:, D_LEAD:])
        nc.sync.dma_start(offs_list[:], offs)
        load_scale_rows(nc.sync, x_scale_table, X_PLANE, x_scales[0])
        nc.sync.dma_start(out=x_table[:], in_=x_words[0].rearrange("p n t -> p (n t)").bitcast(I32))
        nc.sync.dma_start(out=w_codes[:].bitcast(I32), in_=w1_words[0].bitcast(I32))
        load_scale_rows(nc.sync, w_plane, 0, w1_scales[0])
        nc.sync.dma_start(n1_list[:], n1)
        nc.sync.dma_start(n2_list[:], n2)
        nc.sync.dma_start(n3_list[:], n3)

        nc.scalar.activation(out=gain16[:], in_=gain[:], func=COPY, scale=0.0625)

        d_plane = keep.tile([P, CODEWORDS], U8, name="d_plane", align_bytes=64)
        d_codes = keep.tile([P, CODEWORDS], U32, name="d_codes", align_bytes=64)
        x_plane = keep.tile([P, TOKENS], U8, name="x_plane", align_bytes=64)
        nc.vector.tensor_copy(
            out=d_plane[:].rearrange("p (t m) -> p m t", t=PACK), in_=d_scale_table[:].indirect(ci_list[:])
        )
        nc.vector.tensor_copy(
            out=d_codes[:].rearrange("p (t m) -> p m t", t=PACK), in_=d_table[:].bitcast(U32).indirect(ci_list[:])
        )
        nc.vector.tensor_copy(out=x_plane[:], in_=x_scale_table[:].indirect(offs_list[:]))

        z_codes = keep.tile([P, TOKENS], U32, name="z_codes", align_bytes=64)
        z_plane = keep.tile([P, TOKENS], U8, name="z_plane", align_bytes=64)
        h_rows = [keep.tile([P, TOKENS], F32, name="h_rows%d" % b, align_bytes=64) for b in range(BLOCKS)]

        def layer(b, start, count, bank):
            h_bank = psum.tile([P, count], F32, name="h_bank%d_%d" % (b, start), tag=bank)
            nc.tensor.matmul_mx(
                out=h_bank[:],
                lhsT=w_codes[:, 2 * P * b : 2 * P * (b + 1)].bitcast(FP4X4),
                lhsT_scale=w_plane[:, P * b : P * (b + 1)],
                rhs=z_codes[:, start : start + count].bitcast(FP8X4),
                rhs_scale=z_plane[:, start : start + count],
                start=True,
                stop=True,
            )
            nc.vector.tensor_copy(out=h_rows[b][:, start : start + count], in_=h_bank[:])

        for u in range(2):
            tokens = slice(u * HALF, (u + 1) * HALF)
            x_codes = keep.tile([P, HALF], U32, name="x_codes%d" % u, align_bytes=64)
            nc.vector.tensor_copy(
                out=x_codes[:], in_=x_table[:].bitcast(U32).indirect(entries(offs_list, u * HALF, HALF))
            )
            s_bank = psum.tile([P, PACK, HALF], F32, name="s_bank%d" % u, tag="bank%d" % u)
            for t in range(PACK):
                nc.tensor.matmul_mx(
                    out=s_bank[:, t, :],
                    lhsT=d_codes[:, t * P : (t + 1) * P].bitcast(FP8X4),
                    lhsT_scale=d_plane[D_PLANE:P, t * P : (t + 1) * P],
                    rhs=x_codes[:].bitcast(FP8X4),
                    rhs_scale=x_plane[X_PLANE:P, tokens],
                    start=True,
                    stop=True,
                )
            z_half = keep.tile([P, HALF, PACK], BF16, name="z_half%d" % u, align_bytes=64)
            nc.vector.tensor_tensor(
                out=z_half[:],
                in0=s_bank[:].rearrange("p t j -> p j t"),
                in1=gain16[:].unsqueeze(1).to_broadcast([P, HALF, PACK]),
                op=MULT,
            )
            nc.vector.quantize_mx(
                out=z_codes[:, tokens].bitcast(FP8X4),
                scales=z_plane[:, tokens],
                in_=z_half[:].rearrange("p j t -> p (j t)"),
            )
            for b in (0, 1):
                layer(b, u * HALF, HALF, "bank%d" % (1 + 2 * u + b))
        for b in (2, 3):
            layer(b, 0, TOKENS, "bank%d" % (3 + b))

        def scatter(pair, start, count):
            for offsets, factor in ((n1_list, 1.0), (n2_list, 0.5)):
                for b in pair:
                    nc.scalar.activation(
                        out=pages[b][:].indirect(entries(offsets, start, count)),
                        in_=h_rows[b][:, start : start + count],
                        func=COPY,
                        scale=factor,
                    )

        def finish(b, widths):
            start = 0
            for width in widths:
                slots = slice(start, start + width)
                fetched = keep.tile([P, width], F32, name="fetched%d_%d" % (b, start), align_bytes=64)
                nc.scalar.activation(
                    out=fetched[:], in_=pages[b][:].indirect(entries(n3_list, start, width)), func=COPY
                )
                result = keep.tile([P, width], F32, name="result%d_%d" % (b, start), align_bytes=64)
                nc.vector.tensor_tensor(out=result[:], in0=pages[b][:, slots], in1=fetched[:], op=SUBTRACT)
                nc.sync.dma_start(out=out[b * P : (b + 1) * P, slots], in_=result[:])
                start += width

        scatter((0, 1), 0, HALF)
        scatter((0, 1), HALF, HALF)
        finish(0, (256, 256))
        finish(1, (256, 256))
        scatter((2, 3), 0, TOKENS)
        finish(2, (256, 256))
        finish(3, (256, 128, 128))
